import numpy as np
CORES = [401,273,145,17]
N = 4
ROOT = 2
WIDTHS = [256,256,51,512]
XW = 512
def setup_inputs(rng):
    return {"x": rng.standard_normal((N, 128, XW), dtype=np.float32)}
def reference(x):
    g = np.concatenate([x[r][:, :WIDTHS[r]] for r in range(N)], axis=1)
    y = np.full((N, 128, g.shape[1]), np.nan, x.dtype)
    y[ROOT] = g
    return {"y": y}

from concourse.bass import DstId, RemoteDMATransfer

ROOT_RANK = 2
OFF_CHIP = 0x00FF
ON_CHIP_HIGH = 0xFF00
ENGINES = 8

SCRATCH = {
    "land": ("sbuf", [128, 1024], "float32"),
}
SEMAPHORES = ["loaded", "sent", "arr_p0", "arr_p1", "arr_p3a", "arr_p3b", "stored", "own"]


def plan(T):
    widths = T.tables["WIDTHS"]
    cores = T.cores
    root = cores[ROOT_RANK]
    ycol = [sum(widths[:r]) for r in range(len(widths))]

    def lcol(y0):
        return y0 if y0 <= ycol[ROOT_RANK] else y0 - widths[ROOT_RANK]

    half = widths[3] // 2
    cable_relay = cores[1] + 1
    die0_relay = cores[3] + 3
    return {
        "p0": (0, 0, widths[0], ycol[0], lcol(ycol[0]), [cores[0], cable_relay, root]),
        "p1": (1, 0, widths[1], ycol[1], lcol(ycol[1]), [cores[1], root]),
        "p3a": (3, 0, half, ycol[3], lcol(ycol[3]), [cores[3], root]),
        "p3b": (3, half, widths[3] - half, ycol[3] + half, lcol(ycol[3] + half), [cores[3], die0_relay, root]),
    }


def rank_program(g, core, T, topo):
    pieces = plan(T)
    widths = T.tables["WIDTHS"]
    rank = T.rank_of(core)
    land = T.land

    def cols(name):
        l0, w = pieces[name][4], pieces[name][2]
        return land[:, l0:l0 + w]

    def send(name, dst):
        rid, pid = topo.addr(dst, core)
        g.remote_dma(cols(name), cols(name), T.sem["arr_" + name], T.sem.sent, pid, rid, OFF_CHIP)
        g.wait_ge(T.sem.sent, ENGINES)

    if rank == ROOT_RANK:
        y0 = sum(widths[:rank])
        g.dma_start(T.y[:, y0:y0 + widths[rank]], T.x[:, 0:widths[rank]]).then_inc(T.sem.own, 16)
        for q, names in ((g.sync, ("p1", "p0")), (g.scalar, ("p3a", "p3b"))):
            for name in names:
                w, yc = pieces[name][2], pieces[name][3]
                q.wait_ge(T.sem["arr_" + name], ENGINES)
                q.dma_start(T.y[:, yc:yc + w], cols(name)).then_inc(T.sem.stored, 16)
        g.wait_ge(T.sem.own, 16)
        g.wait_ge(T.sem.stored, 16 * len(pieces))
        return

    if rank is not None:
        mine = [n for n in pieces if pieces[n][0] == rank]
        l0 = pieces[mine[0]][4]
        g.sync.dma_start(land[:, l0:l0 + widths[rank]], T.x[:, 0:widths[rank]]).then_inc(T.sem.loaded, 16)
        g.wait_ge(T.sem.loaded, 16)
        if len(mine) == 1:
            send(mine[0], pieces[mine[0]][5][1])
            return
        transfers = []
        for name in mine:
            dst = pieces[name][5][1]
            rid, pid = topo.addr(dst, core)
            on_chip = (topo.host(dst), topo.chip(dst)) == (topo.host(core), topo.chip(core))
            transfers.append(RemoteDMATransfer(
                dst_ids=[DstId(rid=rid, pnc=pid)],
                dma_engine_mask=ON_CHIP_HIGH if on_chip else OFF_CHIP,
                remote_sem=T.sem["arr_" + name],
                src=cols(name), dst=cols(name)))
        g.remote_dma_fused(transfers, local_sem=T.sem.sent)
        g.wait_ge(T.sem.sent, ENGINES * len(transfers))
        return

    for name in pieces:
        way = pieces[name][5]
        if core in way[1:-1]:
            g.wait_ge(T.sem["arr_" + name], ENGINES)
            send(name, way[way.index(core) + 1])
